import numpy as np
import ml_dtypes


def mxq(x, axis, fmt="e4m3"):
    dtype, down = {"e4m3": (ml_dtypes.float8_e4m3fn, 7), "e5m2": (ml_dtypes.float8_e5m2, 14)}[fmt]
    v = np.moveaxis(np.asarray(x, np.float32).astype(ml_dtypes.bfloat16).astype(np.float64), axis, -1)
    blocks = v.reshape(v.shape[:-1] + (-1, 32))
    amax = np.abs(blocks).max(-1, keepdims=True)
    byte = np.maximum(np.where(amax > 0, np.frexp(amax)[1] - 1 + 127, 0) - down, 1)
    scale = np.exp2(byte - 127.0)
    codes = (blocks / scale).astype(np.float32).astype(dtype).astype(np.float64)
    return np.moveaxis((codes * scale).reshape(v.shape), -1, axis)


WIDE = False


def mx_kscale(k, group=512):
    if not WIDE:
        return np.ones(k)
    levels = np.array([18, -18])
    if group != 512:
        return np.exp2(np.random.permutation(np.resize(levels, k // group))).repeat(group)
    if k % 512:
        return np.exp2(np.random.permutation(np.resize(levels, k // 32))).repeat(32)
    a = np.empty((k // 512, 16))
    for p in range(k // 512):
        a[p, :8] = np.random.permutation(np.resize(levels, 8))
        for g in range(8):
            far = levels[np.abs(levels - a[p, g]) >= 10]
            a[p, g + 8] = far[np.random.randint(len(far))]
    return np.exp2(a.ravel()).repeat(32)


def f64(x):
    return np.asarray(x).astype(np.float64)


def sigmoid(v):
    return 1.0 / (1.0 + np.exp(-v))


G, D, M, O, N = 4, 128, 128, 128, 512


def sgn(shape):
    return np.random.uniform(0.5, 2.0, shape) * np.where(np.random.standard_normal(shape) < 0, -1.0, 1.0)


def setup_inputs():
    n = np.random.standard_normal
    s_d = mx_kscale(D, 0)
    s_m = mx_kscale(M, 0)
    return {
        "x": (n((G, D, N)) * s_d[:, None]).astype(np.float32),
        "w1": (n((G, D, M)) / np.sqrt(D) / s_d[:, None]).astype(np.float32),
        "w2": (n((G, D, M)) / np.sqrt(D) / s_d[:, None]).astype(np.float32),
        "th": (np.random.uniform(0.5, 1.5, (G, M, 1))).astype(np.float32),
        "hs": (sgn((G, M, 1)) * s_m[:, None]).astype(np.float32),
        "wo2": (n((G, M, O)) / np.sqrt(M) / s_m[:, None]).astype(np.float32),
        "res": (0.5 * n((G, O, N))).astype(np.float32),
    }


def reference(x, w1, w2, th, hs, wo2, res):
    w1q = mxq(f64(w1), 1, "e4m3")
    xq = mxq(f64(x), 1, "e4m3")
    z1 = w1q.transpose(0, 2, 1) @ xq
    w2q = mxq(f64(w2), 1, "e4m3")
    z2 = w2q.transpose(0, 2, 1) @ xq
    mg = np.sqrt(np.square(z1) + np.square(z2) + 0.05)
    h = mg * sigmoid(mg - f64(th))
    hh = h * f64(hs)
    wo2q = mxq(f64(wo2), 1, "e4m3")
    hhq = mxq(hh, 1, "e4m3")
    y0 = wo2q.transpose(0, 2, 1) @ hhq
    y = y0 + f64(res)
    return y

@@ -1,0 +1,218 @@
+from contextlib import ExitStack
+
+import concourse.mybir as mybir
+
+G, D, M, O, N = 4, 128, 128, 128, 512
+FLOPS = 2 * G * N * (2 * D * M + M * O)
+
+F32 = mybir.dt.float32
+BF16 = mybir.dt.bfloat16
+U32 = mybir.dt.uint32
+U8 = mybir.dt.uint8
+FP8X4 = mybir.dt.float8_e4m3fn_x4
+ACT = mybir.ActivationFunctionType
+ALU = mybir.AluOpType
+
+P = 128
+PACK = 4
+ROWS = 32
+W = 128
+CHUNKS = N // W
+FLOOR = 0.05
+VECTOR_SQUARES = ((2, 3), (3, 3))
+
+
+def tile_rows_fmagnitude_kernel(tc, x, w1, w2, th, hs, wo2, res, out):
+    nc = tc.nc
+    with ExitStack() as ctx:
+        keep = ctx.enter_context(tc.tile_pool(name="keep", bufs=1))
+        psum = ctx.enter_context(tc.psum_pool(name="psum", bufs=1))
+        ctx.enter_context(tc.manual_schedule())
+
+        def sb(name, shape, dtype):
+            return keep.tile(shape, dtype, name=name, align_bytes=64)
+
+        banks = [[psum.tile([P, 512], F32, name="bank%d_%d" % (g, b)) for b in range(2)] for g in range(G)]
+
+        def load_rows(name, src):
+            raw = sb(name, [P, PACK, W], F32)
+            nc.sync.dma_start(out=raw[:], in_=src.rearrange("g (p j) c -> (g p) j c", j=PACK))
+            return raw
+
+        def interleave(name, rows, copy):
+            packed = sb(name, [P, W, PACK], BF16)
+            copy(
+                out=packed[:].rearrange("p (c i) j -> p c j i", i=4),
+                in_=rows[:].rearrange("p j (c i) -> p c j i", i=4),
+            )
+            return packed
+
+        def quantize(name, packed):
+            codes = sb(name + "_codes", [P, W], U32)
+            scales = sb(name + "_scales", [P, W], U8)
+            nc.vector.quantize_mx(
+                out=codes[:].bitcast(FP8X4), scales=scales[:], in_=packed[:].rearrange("p c j -> p (c j)")
+            )
+            return codes, scales
+
+        def product(dst, g, stationary, moving):
+            rows = slice(ROWS * g, ROWS * (g + 1))
+            nc.tensor.matmul_mx(
+                out=dst,
+                lhsT=stationary[0][rows, :].bitcast(FP8X4),
+                lhsT_scale=stationary[1][rows, :],
+                rhs=moving[0][rows, :].bitcast(FP8X4),
+                rhs_scale=moving[1][rows, :],
+                start=True,
+                stop=True,
+            )
+
+        def cols(c):
+            return slice(W * c, W * (c + 1))
+
+        w1_raw = load_rows("w1_raw", w1)
+        w2_raw = load_rows("w2_raw", w2)
+        x_raw = [load_rows("x_raw%d" % c, x[:, :, cols(c)]) for c in range(CHUNKS)]
+        th_t = sb("th_t", [P, PACK], F32)
+        nc.sync.dma_start(out=th_t[:], in_=th.rearrange("g (p j) o -> (g p) (j o)", j=PACK))
+        hs_t = sb("hs_t", [P, PACK], F32)
+        nc.sync.dma_start(out=hs_t[:], in_=hs.rearrange("g (p j) o -> (g p) (j o)", j=PACK))
+        wo_raw = load_rows("wo_raw", wo2)
+        res_t = sb("res_t", [P, G, N], F32)
+        nc.sync.dma_start(out=res_t[:], in_=res.rearrange("g o n -> o g n"))
+
+
+        neg_th = sb("neg_th", [P, PACK], F32)
+        nc.gpsimd.tensor_scalar(out=neg_th[:], in0=th_t[:], scalar1=-1.0, scalar2=0.0, op0=ALU.mult, op1=ALU.add)
+
+        squares = [sb("squares%d" % c, [P, 2, G, W], F32) for c in range(CHUNKS)]
+        sums = [sb("sums%d" % c, [P, G, W], F32) for c in range(CHUNKS)]
+        mg = [sb("mg%d" % c, [P, G, W], F32) for c in range(CHUNKS)]
+        mg_rows = [sb("mg_rows%d" % c, [P, PACK, W], F32) for c in range(CHUNKS)]
+        sig = [sb("sig%d" % c, [P, PACK, W], F32) for c in range(CHUNKS)]
+        hh = [sb("hh%d" % c, [P, PACK, W], BF16) for c in range(CHUNKS)]
+        y = [sb("y%d" % c, [P, G, W], F32) for c in range(CHUNKS)]
+        packed = {}
+        mx = {}
+
+        def cast(name, raw, copy):
+            packed[name] = interleave(name + "_packed", raw, copy)
+
+        def quant(name):
+            mx[name] = quantize(name, packed[name])
+
+        def z_view(c, g):
+            return banks[g][c % 2][:, 2 * W * (c // 2) : 2 * W * (c // 2 + 1)].rearrange("p (r n) -> p r n", r=2)
+
+        def first_layer(c):
+            for r, name in enumerate(("w1", "w2")):
+                for g in range(G):
+                    product(z_view(c, g)[:, r, :], g, mx[name], mx["x%d" % c])
+
+        def scalar_squares(c):
+            for g in range(G):
+                if (c, g) not in VECTOR_SQUARES:
+                    nc.scalar.activation(out=squares[c][:, :, g, :], in_=z_view(c, g), func=ACT.Square)
+
+        def vector_squares(c):
+            for g in range(G):
+                if (c, g) in VECTOR_SQUARES:
+                    z_copy = sb("z_copy%d_%d" % (c, g), [P, 2, W], F32)
+                    nc.vector.tensor_copy(out=z_copy[:], in_=z_view(c, g))
+                    nc.vector.tensor_tensor(out=squares[c][:, :, g, :], in0=z_view(c, g), in1=z_copy[:], op=ALU.mult)
+
+        def add_squares(c):
+            nc.vector.scalar_tensor_tensor(
+                out=sums[c][:], in0=squares[c][:, 0], scalar=FLOOR, in1=squares[c][:, 1], op0=ALU.add, op1=ALU.add
+            )
+
+        def root(c):
+            nc.scalar.activation(out=mg[c][:], in_=sums[c][:], func=ACT.Sqrt)
+            for g in range(G):
+                nc.sync.dma_start(out=mg_rows[c][ROWS * g : ROWS * (g + 1)], in_=mg[c][:, g, :])
+
+        def gate(c):
+            for j in range(PACK):
+                nc.scalar.activation(
+                    out=sig[c][:, j, :], in_=mg_rows[c][:, j, :], func=ACT.Sigmoid, bias=neg_th[:, j : j + 1]
+                )
+
+        def hidden(c):
+            for j in range(PACK):
+                nc.vector.scalar_tensor_tensor(
+                    out=hh[c][:, j, :],
+                    in0=mg_rows[c][:, j, :],
+                    scalar=hs_t[:, j : j + 1],
+                    in1=sig[c][:, j, :],
+                    op0=ALU.mult,
+                    op1=ALU.mult,
+                )
+
+        def second_layer(c):
+            for g in range(G):
+                product(banks[g][c % 2][:, cols(c)], g, mx["wo"], mx["h%d" % c])
+
+        def finish(c):
+            for g in range(G):
+                nc.vector.tensor_tensor(
+                    out=y[c][:, g, :], in0=banks[g][c % 2][:, cols(c)], in1=res_t[:, g, cols(c)], op=ALU.add
+                )
+            nc.sync.dma_start(out=out[:, :, cols(c)].rearrange("g o n -> o g n"), in_=y[c][:])
+
+        on_vector, on_scalar = nc.vector.tensor_copy, nc.scalar.copy
+        cast("w1", w1_raw, on_vector)
+        cast("w2", w2_raw, on_vector)
+        quant("w1")
+        cast("x0", x_raw[0], on_vector)
+        quant("w2")
+        quant("x0")
+        first_layer(0)
+        cast("x1", x_raw[1], on_vector)
+        quant("x1")
+        first_layer(1)
+        scalar_squares(0)
+        cast("x2", x_raw[2], on_vector)
+        quant("x2")
+        first_layer(2)
+        cast("x3", x_raw[3], on_vector)
+        add_squares(0)
+        scalar_squares(1)
+        quant("x3")
+        first_layer(3)
+        root(0)
+        vector_squares(2)
+        add_squares(1)
+        scalar_squares(2)
+        root(1)
+        vector_squares(3)
+        scalar_squares(3)
+        add_squares(2)
+        add_squares(3)
+        root(2)
+        root(3)
+        cast("wo", wo_raw, on_vector)
+        quant("wo")
+        gate(0)
+        hidden(0)
+        gate(1)
+        cast("h0", hh[0], on_vector)
+        hidden(1)
+        quant("h0")
+        second_layer(0)
+        gate(2)
+        gate(3)
+        hidden(2)
+        cast("h1", hh[1], on_scalar)
+        hidden(3)
+        cast("h2", hh[2], on_scalar)
+        quant("h1")
+        second_layer(1)
+        finish(0)
+        cast("h3", hh[3], on_scalar)
+        quant("h2")
+        second_layer(2)
+        finish(1)
+        quant("h3")
+        second_layer(3)
+        finish(2)
+        finish(3)

@@ -18,8 +18,10 @@ PACK = 4
 ROWS = 32
 W = 128
 CHUNKS = N // W
+LAST = CHUNKS - 1
+BANK = 512
+RUN = 4
 FLOOR = 0.05
-VECTOR_SQUARES = ((2, 3), (3, 3))
 
 
 def tile_rows_fmagnitude_kernel(tc, x, w1, w2, th, hs, wo2, res, out):
@@ -29,190 +31,194 @@ def tile_rows_fmagnitude_kernel(tc, x, w1, w2, th, hs, wo2, res, out):
         psum = ctx.enter_context(tc.psum_pool(name="psum", bufs=1))
         ctx.enter_context(tc.manual_schedule())
 
-        def sb(name, shape, dtype):
+        def sbuf(name, shape, dtype):
             return keep.tile(shape, dtype, name=name, align_bytes=64)
 
-        banks = [[psum.tile([P, 512], F32, name="bank%d_%d" % (g, b)) for b in range(2)] for g in range(G)]
+        def per_chunk(name, shape, dtype):
+            return [sbuf("%s%d" % (name, c), shape, dtype) for c in range(CHUNKS)]
+
+        def cols(c):
+            return slice(W * c, W * (c + 1))
+
+        banks = [[psum.tile([P, BANK], F32, name="bank%d_%d" % (g, b)) for b in range(2)] for g in range(G)]
+
+        def z_sums(c, g):
+            first = 2 * W * (c // 2)
+            return banks[g][c % 2][:, first : first + 2 * W].rearrange("p (r n) -> p r n", r=2)
+
+        def y_sums(c, g):
+            return banks[g][c % 2][:, cols(c)]
 
         def load_rows(name, src):
-            raw = sb(name, [P, PACK, W], F32)
-            nc.sync.dma_start(out=raw[:], in_=src.rearrange("g (p j) c -> (g p) j c", j=PACK))
-            return raw
+            rows = sbuf(name, [P, PACK, src.shape[2]], F32)
+            nc.sync.dma_start(out=rows[:], in_=src.rearrange("g (p j) c -> (g p) j c", j=PACK))
+            return rows
 
-        def interleave(name, rows, copy):
-            packed = sb(name, [P, W, PACK], BF16)
+        w1_rows = load_rows("w1_rows", w1)
+        x_rows = [load_rows("x_rows0", x[:, :, cols(0)])]
+        w2_rows = load_rows("w2_rows", w2)
+        x_rows.extend(load_rows("x_rows%d" % c, x[:, :, cols(c)]) for c in range(1, CHUNKS))
+        th_rows = load_rows("th_rows", th)
+        hs_rows = load_rows("hs_rows", hs)
+        wo_rows = load_rows("wo_rows", wo2)
+        res_sb = sbuf("res_sb", [P, G, N], F32)
+        nc.sync.dma_start(out=res_sb[:], in_=res.rearrange("g o n -> o g n"))
+
+        warm_in = sbuf("warm_in", [P, 1], F32)
+        warm_out = sbuf("warm_out", [P, 1], F32)
+        nc.gpsimd.memset(warm_in[:], 1.0)
+        nc.scalar.activation(out=warm_out[:], in_=warm_in[:], func=ACT.Sqrt)
+
+        on_vector, on_scalar = nc.vector.tensor_copy, nc.scalar.copy
+
+        def pack(packed, rows, copy):
             copy(
-                out=packed[:].rearrange("p (c i) j -> p c j i", i=4),
-                in_=rows[:].rearrange("p j (c i) -> p c j i", i=4),
+                out=packed.rearrange("p (c i) j -> p c j i", i=RUN),
+                in_=rows.rearrange("p j (c i) -> p c j i", i=RUN),
             )
-            return packed
 
         def quantize(name, packed):
-            codes = sb(name + "_codes", [P, W], U32)
-            scales = sb(name + "_scales", [P, W], U8)
+            codes = sbuf(name + "_codes", [P, W], U32)
+            scales = sbuf(name + "_scales", [P, W], U8)
             nc.vector.quantize_mx(
                 out=codes[:].bitcast(FP8X4), scales=scales[:], in_=packed[:].rearrange("p c j -> p (c j)")
             )
             return codes, scales
 
-        def product(dst, g, stationary, moving):
-            rows = slice(ROWS * g, ROWS * (g + 1))
+        def product(sums, g, weights, moving):
+            tile_rows = slice(ROWS * g, ROWS * (g + 1))
             nc.tensor.matmul_mx(
-                out=dst,
-                lhsT=stationary[0][rows, :].bitcast(FP8X4),
-                lhsT_scale=stationary[1][rows, :],
-                rhs=moving[0][rows, :].bitcast(FP8X4),
-                rhs_scale=moving[1][rows, :],
+                out=sums,
+                lhsT=weights[0][tile_rows, :].bitcast(FP8X4),
+                lhsT_scale=weights[1][tile_rows, :],
+                rhs=moving[0][tile_rows, :].bitcast(FP8X4),
+                rhs_scale=moving[1][tile_rows, :],
                 start=True,
                 stop=True,
             )
 
-        def cols(c):
-            return slice(W * c, W * (c + 1))
+        w1_packed = sbuf("w1_packed", [P, W, PACK], BF16)
+        w2_packed = sbuf("w2_packed", [P, W, PACK], BF16)
+        wo_packed = sbuf("wo_packed", [P, W, PACK], BF16)
+        x_packed = per_chunk("x_packed", [P, W, PACK], BF16)
+        hh_packed = per_chunk("hh_packed", [P, W, PACK], BF16)
 
-        w1_raw = load_rows("w1_raw", w1)
-        w2_raw = load_rows("w2_raw", w2)
-        x_raw = [load_rows("x_raw%d" % c, x[:, :, cols(c)]) for c in range(CHUNKS)]
-        th_t = sb("th_t", [P, PACK], F32)
-        nc.sync.dma_start(out=th_t[:], in_=th.rearrange("g (p j) o -> (g p) (j o)", j=PACK))
-        hs_t = sb("hs_t", [P, PACK], F32)
-        nc.sync.dma_start(out=hs_t[:], in_=hs.rearrange("g (p j) o -> (g p) (j o)", j=PACK))
-        wo_raw = load_rows("wo_raw", wo2)
-        res_t = sb("res_t", [P, G, N], F32)
-        nc.sync.dma_start(out=res_t[:], in_=res.rearrange("g o n -> o g n"))
+        squares = per_chunk("squares", [P, 2, G, W], F32)
+        radicand = per_chunk("radicand", [P, G, W], F32)
+        mg = per_chunk("mg", [P, G, W], F32)
+        mg_rows = per_chunk("mg_rows", [P, PACK, W], F32)
 
+        def vector_groups(c):
+            return range(G - max(c - 1, 0), G)
 
-        neg_th = sb("neg_th", [P, PACK], F32)
-        nc.gpsimd.tensor_scalar(out=neg_th[:], in0=th_t[:], scalar1=-1.0, scalar2=0.0, op0=ALU.mult, op1=ALU.add)
-
-        squares = [sb("squares%d" % c, [P, 2, G, W], F32) for c in range(CHUNKS)]
-        sums = [sb("sums%d" % c, [P, G, W], F32) for c in range(CHUNKS)]
-        mg = [sb("mg%d" % c, [P, G, W], F32) for c in range(CHUNKS)]
-        mg_rows = [sb("mg_rows%d" % c, [P, PACK, W], F32) for c in range(CHUNKS)]
-        sig = [sb("sig%d" % c, [P, PACK, W], F32) for c in range(CHUNKS)]
-        hh = [sb("hh%d" % c, [P, PACK, W], BF16) for c in range(CHUNKS)]
-        y = [sb("y%d" % c, [P, G, W], F32) for c in range(CHUNKS)]
-        packed = {}
-        mx = {}
-
-        def cast(name, raw, copy):
-            packed[name] = interleave(name + "_packed", raw, copy)
-
-        def quant(name):
-            mx[name] = quantize(name, packed[name])
-
-        def z_view(c, g):
-            return banks[g][c % 2][:, 2 * W * (c // 2) : 2 * W * (c // 2 + 1)].rearrange("p (r n) -> p r n", r=2)
-
-        def first_layer(c):
-            for r, name in enumerate(("w1", "w2")):
-                for g in range(G):
-                    product(z_view(c, g)[:, r, :], g, mx[name], mx["x%d" % c])
-
-        def scalar_squares(c):
-            for g in range(G):
-                if (c, g) not in VECTOR_SQUARES:
-                    nc.scalar.activation(out=squares[c][:, :, g, :], in_=z_view(c, g), func=ACT.Square)
-
-        def vector_squares(c):
-            for g in range(G):
-                if (c, g) in VECTOR_SQUARES:
-                    z_copy = sb("z_copy%d_%d" % (c, g), [P, 2, W], F32)
-                    nc.vector.tensor_copy(out=z_copy[:], in_=z_view(c, g))
-                    nc.vector.tensor_tensor(out=squares[c][:, :, g, :], in0=z_view(c, g), in1=z_copy[:], op=ALU.mult)
-
-        def add_squares(c):
+        def add_squares(c, groups):
             nc.vector.scalar_tensor_tensor(
-                out=sums[c][:], in0=squares[c][:, 0], scalar=FLOOR, in1=squares[c][:, 1], op0=ALU.add, op1=ALU.add
+                out=radicand[c][:, groups, :],
+                in0=squares[c][:, 0, groups, :],
+                scalar=FLOOR,
+                in1=squares[c][:, 1, groups, :],
+                op0=ALU.add,
+                op1=ALU.add,
             )
 
-        def root(c):
-            nc.scalar.activation(out=mg[c][:], in_=sums[c][:], func=ACT.Sqrt)
-            for g in range(G):
+        def root(c, groups):
+            nc.scalar.activation(out=mg[c][:, groups, :], in_=radicand[c][:, groups, :], func=ACT.Sqrt)
+            for g in sorted(range(groups.start, groups.stop), key=lambda k: k % 2):
                 nc.sync.dma_start(out=mg_rows[c][ROWS * g : ROWS * (g + 1)], in_=mg[c][:, g, :])
 
-        def gate(c):
-            for j in range(PACK):
-                nc.scalar.activation(
-                    out=sig[c][:, j, :], in_=mg_rows[c][:, j, :], func=ACT.Sigmoid, bias=neg_th[:, j : j + 1]
-                )
+        pack(w1_packed[:], w1_rows[:], on_vector)
+        pack(x_packed[0][:], x_rows[0][:], on_vector)
+        w1_mx = quantize("w1", w1_packed)
+        x_mx = quantize("x0", x_packed[0])
+        for g in range(G):
+            product(z_sums(0, g)[:, 0, :], g, w1_mx, x_mx)
+        half = W // 2
+        pack(w2_packed[:, :half, :], w2_rows[:, :, :half], on_scalar)
+        pack(w2_packed[:, half:, :], w2_rows[:, :, half:], on_vector)
+        w2_mx = quantize("w2", w2_packed)
+        for g in range(G):
+            nc.scalar.activation(out=squares[0][:, 0, g, :], in_=z_sums(0, g)[:, 0, :], func=ACT.Square)
+        for g in range(G):
+            product(z_sums(0, g)[:, 1, :], g, w2_mx, x_mx)
+        for g in range(G):
+            nc.scalar.activation(out=squares[0][:, 1, g, :], in_=z_sums(0, g)[:, 1, :], func=ACT.Square)
+
+        all_groups = slice(0, G)
+        for c in range(-1, CHUNKS):
+            ahead = c + 2
+            if ahead < CHUNKS:
+                pack(x_packed[ahead][:], x_rows[ahead][:], on_vector)
+            if c >= 1:
+                z_copy = {g: sbuf("z_copy%d_%d" % (c, g), [P, 2, W], F32) for g in vector_groups(c)}
+                for g, copied in z_copy.items():
+                    nc.vector.tensor_copy(out=copied[:], in_=z_sums(c, g))
+                add_squares(c - 1, all_groups)
+                for g in range(vector_groups(c).start):
+                    nc.scalar.activation(out=squares[c][:, :, g, :], in_=z_sums(c, g), func=ACT.Square)
+                root(c - 1, all_groups)
+                for g, copied in z_copy.items():
+                    nc.vector.tensor_tensor(out=squares[c][:, :, g, :], in0=copied[:], in1=copied[:], op=ALU.mult)
+            if ahead < CHUNKS:
+                x_mx = quantize("x%d" % ahead, x_packed[ahead])
+                for r, weights in enumerate((w1_mx, w2_mx)):
+                    for g in range(G):
+                        product(z_sums(ahead, g)[:, r, :], g, weights, x_mx)
+        for groups in (slice(0, G // 2), slice(G // 2, G)):
+            add_squares(LAST, groups)
+            root(LAST, groups)
+
+        neg_th = sbuf("neg_th", [P, PACK, 1], F32)
+        nc.vector.tensor_scalar(out=neg_th[:], in0=th_rows[:], scalar1=-1.0, scalar2=None, op0=ALU.mult)
+        pack(wo_packed[:], wo_rows[:], on_vector)
+        wo_mx = quantize("wo", wo_packed)
+
+        gate = per_chunk("gate", [P, PACK, W], F32)
+        hh_rows = per_chunk("hh_rows", [P, PACK, W], BF16)
+        out_sb = per_chunk("out_sb", [P, G, W], F32)
 
         def hidden(c):
             for j in range(PACK):
+                nc.scalar.activation(
+                    out=gate[c][:, j, :], in_=mg_rows[c][:, j, :], func=ACT.Sigmoid, bias=neg_th[:, j, :]
+                )
+            for j in range(PACK):
                 nc.vector.scalar_tensor_tensor(
-                    out=hh[c][:, j, :],
+                    out=hh_rows[c][:, j, :],
                     in0=mg_rows[c][:, j, :],
-                    scalar=hs_t[:, j : j + 1],
-                    in1=sig[c][:, j, :],
+                    scalar=hs_rows[:, j, :],
+                    in1=gate[c][:, j, :],
                     op0=ALU.mult,
                     op1=ALU.mult,
                 )
 
-        def second_layer(c):
+        def second_product(c):
+            hh_mx = quantize("hh%d" % c, hh_packed[c])
             for g in range(G):
-                product(banks[g][c % 2][:, cols(c)], g, mx["wo"], mx["h%d" % c])
+                product(y_sums(c, g), g, wo_mx, hh_mx)
 
         def finish(c):
+            stored = 1 if c == LAST else 2
             for g in range(G):
                 nc.vector.tensor_tensor(
-                    out=y[c][:, g, :], in0=banks[g][c % 2][:, cols(c)], in1=res_t[:, g, cols(c)], op=ALU.add
+                    out=out_sb[c][:, g, :], in0=y_sums(c, g), in1=res_sb[:, g, cols(c)], op=ALU.add
                 )
-            nc.sync.dma_start(out=out[:, :, cols(c)].rearrange("g o n -> o g n"), in_=y[c][:])
+                if (g + 1) % stored == 0:
+                    groups = slice(g + 1 - stored, g + 1)
+                    nc.sync.dma_start(
+                        out=out[groups, :, cols(c)].rearrange("g o n -> o g n"), in_=out_sb[c][:, groups, :]
+                    )
 
-        on_vector, on_scalar = nc.vector.tensor_copy, nc.scalar.copy
-        cast("w1", w1_raw, on_vector)
-        cast("w2", w2_raw, on_vector)
-        quant("w1")
-        cast("x0", x_raw[0], on_vector)
-        quant("w2")
-        quant("x0")
-        first_layer(0)
-        cast("x1", x_raw[1], on_vector)
-        quant("x1")
-        first_layer(1)
-        scalar_squares(0)
-        cast("x2", x_raw[2], on_vector)
-        quant("x2")
-        first_layer(2)
-        cast("x3", x_raw[3], on_vector)
-        add_squares(0)
-        scalar_squares(1)
-        quant("x3")
-        first_layer(3)
-        root(0)
-        vector_squares(2)
-        add_squares(1)
-        scalar_squares(2)
-        root(1)
-        vector_squares(3)
-        scalar_squares(3)
-        add_squares(2)
-        add_squares(3)
-        root(2)
-        root(3)
-        cast("wo", wo_raw, on_vector)
-        quant("wo")
-        gate(0)
         hidden(0)
-        gate(1)
-        cast("h0", hh[0], on_vector)
         hidden(1)
-        quant("h0")
-        second_layer(0)
-        gate(2)
-        gate(3)
+        pack(hh_packed[0][:], hh_rows[0][:], on_vector)
         hidden(2)
-        cast("h1", hh[1], on_scalar)
-        hidden(3)
-        cast("h2", hh[2], on_scalar)
-        quant("h1")
-        second_layer(1)
-        finish(0)
-        cast("h3", hh[3], on_scalar)
-        quant("h2")
-        second_layer(2)
-        finish(1)
-        quant("h3")
-        second_layer(3)
-        finish(2)
-        finish(3)
+        pack(hh_packed[1][:], hh_rows[1][:], on_scalar)
+        second_product(0)
+        second_product(1)
+        hidden(LAST)
+        for c in range(2, CHUNKS):
+            pack(hh_packed[c][:], hh_rows[c][:], on_scalar)
+            finish(c - 2)
+            second_product(c)
+        finish(LAST - 1)
+        finish(LAST)

@@ -61,8 +61,13 @@ def tile_rows_fmagnitude_kernel(tc, x, w1, w2, th, hs, wo2, res, out):
         th_rows = load_rows("th_rows", th)
         hs_rows = load_rows("hs_rows", hs)
         wo_rows = load_rows("wo_rows", wo2)
-        res_sb = sbuf("res_sb", [P, G, N], F32)
-        nc.sync.dma_start(out=res_sb[:], in_=res.rearrange("g o n -> o g n"))
+
+        def load_res(h):
+            part = sbuf("res_half%d" % h, [P, G, 2 * W], F32)
+            nc.sync.dma_start(out=part[:], in_=res[:, :, 2 * W * h : 2 * W * (h + 1)].rearrange("g o n -> o g n"))
+            return part
+
+        res_halves = [load_res(0)]
 
         warm_in = sbuf("warm_in", [P, 1], F32)
         warm_out = sbuf("warm_out", [P, 1], F32)
@@ -166,6 +171,7 @@ def tile_rows_fmagnitude_kernel(tc, x, w1, w2, th, hs, wo2, res, out):
         for groups in (slice(0, G // 2), slice(G // 2, G)):
             add_squares(LAST, groups)
             root(LAST, groups)
+        res_halves.append(load_res(1))
 
         neg_th = sbuf("neg_th", [P, PACK, 1], F32)
         nc.vector.tensor_scalar(out=neg_th[:], in0=th_rows[:], scalar1=-1.0, scalar2=None, op0=ALU.mult)
@@ -197,11 +203,10 @@ def tile_rows_fmagnitude_kernel(tc, x, w1, w2, th, hs, wo2, res, out):
                 product(y_sums(c, g), g, wo_mx, hh_mx)
 
         def finish(c):
-            stored = 1 if c == LAST else 2
+            stored = 1 if c in (0, LAST) else 2
             for g in range(G):
-                nc.vector.tensor_tensor(
-                    out=out_sb[c][:, g, :], in0=y_sums(c, g), in1=res_sb[:, g, cols(c)], op=ALU.add
-                )
+                residual = res_halves[c // 2][:, g, cols(c % 2)]
+                nc.vector.tensor_tensor(out=out_sb[c][:, g, :], in0=y_sums(c, g), in1=residual, op=ALU.add)
                 if (g + 1) % stored == 0:
                     groups = slice(g + 1 - stored, g + 1)
                     nc.sync.dma_start(

from contextlib import ExitStack

import concourse.mybir as mybir

G, D, M, O, N = 4, 128, 128, 128, 512
FLOPS = 2 * G * N * (2 * D * M + M * O)

F32 = mybir.dt.float32
BF16 = mybir.dt.bfloat16
U32 = mybir.dt.uint32
U8 = mybir.dt.uint8
FP8X4 = mybir.dt.float8_e4m3fn_x4
ACT = mybir.ActivationFunctionType
ALU = mybir.AluOpType

P = 128
PACK = 4
ROWS = 32
W = 128
CHUNKS = N // W
LAST = CHUNKS - 1
BANK = 512
RUN = 4
FLOOR = 0.05


def tile_rows_fmagnitude_kernel(tc, x, w1, w2, th, hs, wo2, res, out):
    nc = tc.nc
    with ExitStack() as ctx:
        keep = ctx.enter_context(tc.tile_pool(name="keep", bufs=1))
        psum = ctx.enter_context(tc.psum_pool(name="psum", bufs=1))
        ctx.enter_context(tc.manual_schedule())

        def sbuf(name, shape, dtype):
            return keep.tile(shape, dtype, name=name, align_bytes=64)

        def per_chunk(name, shape, dtype):
            return [sbuf("%s%d" % (name, c), shape, dtype) for c in range(CHUNKS)]

        def cols(c):
            return slice(W * c, W * (c + 1))

        banks = [[psum.tile([P, BANK], F32, name="bank%d_%d" % (g, b)) for b in range(2)] for g in range(G)]

        def z_sums(c, g):
            first = 2 * W * (c // 2)
            return banks[g][c % 2][:, first : first + 2 * W].rearrange("p (r n) -> p r n", r=2)

        def y_sums(c, g):
            return banks[g][c % 2][:, cols(c)]

        def load_rows(name, src):
            rows = sbuf(name, [P, PACK, src.shape[2]], F32)
            nc.sync.dma_start(out=rows[:], in_=src.rearrange("g (p j) c -> (g p) j c", j=PACK))
            return rows

        w1_rows = load_rows("w1_rows", w1)
        x_rows = [load_rows("x_rows0", x[:, :, cols(0)])]
        w2_rows = load_rows("w2_rows", w2)
        x_rows.extend(load_rows("x_rows%d" % c, x[:, :, cols(c)]) for c in range(1, CHUNKS))
        th_rows = load_rows("th_rows", th)
        hs_rows = load_rows("hs_rows", hs)
        wo_rows = load_rows("wo_rows", wo2)

        def load_res(h):
            part = sbuf("res_half%d" % h, [P, G, 2 * W], F32)
            nc.sync.dma_start(out=part[:], in_=res[:, :, 2 * W * h : 2 * W * (h + 1)].rearrange("g o n -> o g n"))
            return part

        res_halves = [load_res(0)]

        warm_in = sbuf("warm_in", [P, 1], F32)
        warm_out = sbuf("warm_out", [P, 1], F32)
        nc.gpsimd.memset(warm_in[:], 1.0)
        nc.scalar.activation(out=warm_out[:], in_=warm_in[:], func=ACT.Sqrt)

        on_vector, on_scalar = nc.vector.tensor_copy, nc.scalar.copy

        def pack(packed, rows, copy):
            copy(
                out=packed.rearrange("p (c i) j -> p c j i", i=RUN),
                in_=rows.rearrange("p j (c i) -> p c j i", i=RUN),
            )

        def quantize(name, packed):
            codes = sbuf(name + "_codes", [P, W], U32)
            scales = sbuf(name + "_scales", [P, W], U8)
            nc.vector.quantize_mx(
                out=codes[:].bitcast(FP8X4), scales=scales[:], in_=packed[:].rearrange("p c j -> p (c j)")
            )
            return codes, scales

        def product(sums, g, weights, moving):
            tile_rows = slice(ROWS * g, ROWS * (g + 1))
            nc.tensor.matmul_mx(
                out=sums,
                lhsT=weights[0][tile_rows, :].bitcast(FP8X4),
                lhsT_scale=weights[1][tile_rows, :],
                rhs=moving[0][tile_rows, :].bitcast(FP8X4),
                rhs_scale=moving[1][tile_rows, :],
                start=True,
                stop=True,
            )

        w1_packed = sbuf("w1_packed", [P, W, PACK], BF16)
        w2_packed = sbuf("w2_packed", [P, W, PACK], BF16)
        wo_packed = sbuf("wo_packed", [P, W, PACK], BF16)
        x_packed = per_chunk("x_packed", [P, W, PACK], BF16)
        hh_packed = per_chunk("hh_packed", [P, W, PACK], BF16)

        squares = per_chunk("squares", [P, 2, G, W], F32)
        radicand = per_chunk("radicand", [P, G, W], F32)
        mg = per_chunk("mg", [P, G, W], F32)
        mg_rows = per_chunk("mg_rows", [P, PACK, W], F32)

        def vector_groups(c):
            return range(G - max(c - 1, 0), G)

        def add_squares(c, groups):
            nc.vector.scalar_tensor_tensor(
                out=radicand[c][:, groups, :],
                in0=squares[c][:, 0, groups, :],
                scalar=FLOOR,
                in1=squares[c][:, 1, groups, :],
                op0=ALU.add,
                op1=ALU.add,
            )

        def root(c, groups):
            nc.scalar.activation(out=mg[c][:, groups, :], in_=radicand[c][:, groups, :], func=ACT.Sqrt)
            for g in sorted(range(groups.start, groups.stop), key=lambda k: k % 2):
                nc.sync.dma_start(out=mg_rows[c][ROWS * g : ROWS * (g + 1)], in_=mg[c][:, g, :])

        pack(w1_packed[:], w1_rows[:], on_vector)
        pack(x_packed[0][:], x_rows[0][:], on_vector)
        w1_mx = quantize("w1", w1_packed)
        x_mx = quantize("x0", x_packed[0])
        for g in range(G):
            product(z_sums(0, g)[:, 0, :], g, w1_mx, x_mx)
        half = W // 2
        pack(w2_packed[:, :half, :], w2_rows[:, :, :half], on_scalar)
        pack(w2_packed[:, half:, :], w2_rows[:, :, half:], on_vector)
        w2_mx = quantize("w2", w2_packed)
        for g in range(G):
            nc.scalar.activation(out=squares[0][:, 0, g, :], in_=z_sums(0, g)[:, 0, :], func=ACT.Square)
        for g in range(G):
            product(z_sums(0, g)[:, 1, :], g, w2_mx, x_mx)
        for g in range(G):
            nc.scalar.activation(out=squares[0][:, 1, g, :], in_=z_sums(0, g)[:, 1, :], func=ACT.Square)

        all_groups = slice(0, G)
        for c in range(-1, CHUNKS):
            ahead = c + 2
            if ahead < CHUNKS:
                pack(x_packed[ahead][:], x_rows[ahead][:], on_vector)
            if c >= 1:
                z_copy = {g: sbuf("z_copy%d_%d" % (c, g), [P, 2, W], F32) for g in vector_groups(c)}
                for g, copied in z_copy.items():
                    nc.vector.tensor_copy(out=copied[:], in_=z_sums(c, g))
                add_squares(c - 1, all_groups)
                for g in range(vector_groups(c).start):
                    nc.scalar.activation(out=squares[c][:, :, g, :], in_=z_sums(c, g), func=ACT.Square)
                root(c - 1, all_groups)
                for g, copied in z_copy.items():
                    nc.vector.tensor_tensor(out=squares[c][:, :, g, :], in0=copied[:], in1=copied[:], op=ALU.mult)
            if ahead < CHUNKS:
                x_mx = quantize("x%d" % ahead, x_packed[ahead])
                for r, weights in enumerate((w1_mx, w2_mx)):
                    for g in range(G):
                        product(z_sums(ahead, g)[:, r, :], g, weights, x_mx)
        for groups in (slice(0, G // 2), slice(G // 2, G)):
            add_squares(LAST, groups)
            root(LAST, groups)
        res_halves.append(load_res(1))

        neg_th = sbuf("neg_th", [P, PACK, 1], F32)
        nc.vector.tensor_scalar(out=neg_th[:], in0=th_rows[:], scalar1=-1.0, scalar2=None, op0=ALU.mult)
        pack(wo_packed[:], wo_rows[:], on_vector)
        wo_mx = quantize("wo", wo_packed)

        gate = per_chunk("gate", [P, PACK, W], F32)
        hh_rows = per_chunk("hh_rows", [P, PACK, W], BF16)
        out_sb = per_chunk("out_sb", [P, G, W], F32)

        def hidden(c):
            for j in range(PACK):
                nc.scalar.activation(
                    out=gate[c][:, j, :], in_=mg_rows[c][:, j, :], func=ACT.Sigmoid, bias=neg_th[:, j, :]
                )
            for j in range(PACK):
                nc.vector.scalar_tensor_tensor(
                    out=hh_rows[c][:, j, :],
                    in0=mg_rows[c][:, j, :],
                    scalar=hs_rows[:, j, :],
                    in1=gate[c][:, j, :],
                    op0=ALU.mult,
                    op1=ALU.mult,
                )

        def second_product(c):
            hh_mx = quantize("hh%d" % c, hh_packed[c])
            for g in range(G):
                product(y_sums(c, g), g, wo_mx, hh_mx)

        def finish(c):
            stored = 1 if c in (0, LAST) else 2
            for g in range(G):
                residual = res_halves[c // 2][:, g, cols(c % 2)]
                nc.vector.tensor_tensor(out=out_sb[c][:, g, :], in0=y_sums(c, g), in1=residual, op=ALU.add)
                if (g + 1) % stored == 0:
                    groups = slice(g + 1 - stored, g + 1)
                    nc.sync.dma_start(
                        out=out[groups, :, cols(c)].rearrange("g o n -> o g n"), in_=out_sb[c][:, groups, :]
                    )

        hidden(0)
        hidden(1)
        pack(hh_packed[0][:], hh_rows[0][:], on_vector)
        hidden(2)
        pack(hh_packed[1][:], hh_rows[1][:], on_scalar)
        second_product(0)
        second_product(1)
        hidden(LAST)
        for c in range(2, CHUNKS):
            pack(hh_packed[c][:], hh_rows[c][:], on_scalar)
            finish(c - 2)
            second_product(c)
        finish(LAST - 1)
        finish(LAST)
